import numpy as np
import ml_dtypes


def mxq(x, axis, fmt="e4m3"):
    dtype, down = {"e4m3": (ml_dtypes.float8_e4m3fn, 7), "e5m2": (ml_dtypes.float8_e5m2, 14)}[fmt]
    v = np.moveaxis(np.asarray(x, np.float32).astype(ml_dtypes.bfloat16).astype(np.float64), axis, -1)
    blocks = v.reshape(v.shape[:-1] + (-1, 32))
    amax = np.abs(blocks).max(-1, keepdims=True)
    byte = np.maximum(np.where(amax > 0, np.frexp(amax)[1] - 1 + 127, 0) - down, 1)
    scale = np.exp2(byte - 127.0)
    codes = (blocks / scale).astype(np.float32).astype(dtype).astype(np.float64)
    return np.moveaxis((codes * scale).reshape(v.shape), -1, axis)


WIDE = False


def mx_kscale(k):
    if not WIDE:
        return np.ones(k)
    levels = np.array([10, -10, 5, -5, 0])
    if k % 512:
        return np.exp2(np.random.permutation(np.resize(levels, k // 32))).repeat(32)
    a = np.empty((k // 512, 16))
    for p in range(k // 512):
        a[p, :8] = np.random.permutation(np.resize(levels, 8))
        for g in range(8):
            far = levels[np.abs(levels - a[p, g]) >= 10]
            a[p, g + 8] = far[np.random.randint(len(far))]
    return np.exp2(a.ravel()).repeat(32)


BF16 = ml_dtypes.bfloat16


def bf(x):
    return np.asarray(x, np.float32).astype(BF16)


def f64(x):
    return np.asarray(x).astype(np.float64)


E2M1 = np.array([0.0, 0.5, 1.0, 1.5, 2.0, 3.0, 4.0, 6.0, -0.0, -0.5, -1.0, -1.5, -2.0, -3.0, -4.0, -6.0])


def pack_weight(w, fmt):
    k, n = w.shape
    w = f64(bf(w)).reshape(k // 32, 32, n)
    amax = np.abs(w).max(1)
    if fmt == "e4m3":
        byte = np.frexp(amax)[1] - 1 + 127 - 7
    else:
        mant, ex = np.frexp(amax / 6.0)
        byte = np.where(mant > 0.5, ex, ex - 1) + 127
    byte = np.clip(np.where(amax > 0, byte, 1), 1, 254)
    scaled = (w * np.exp2(127.0 - byte)[:, None, :]).reshape(k, n).astype(np.float32)
    by_word = np.ascontiguousarray(scaled.reshape(k // 512, 128, 4, n).transpose(0, 1, 3, 2))
    if fmt == "e4m3":
        words = by_word.astype(ml_dtypes.float8_e4m3fn).view(np.uint8)
    else:
        c = by_word.astype(ml_dtypes.float4_e2m1fn).view(np.uint8) & 0xF
        words = c[..., 0::2] | (c[..., 1::2] << 4)
    return np.ascontiguousarray(words), np.ascontiguousarray(byte.astype(np.uint8).reshape(k // 512, 16, n))


def unpack_weight(words, scales, fmt):
    g, p, n, _ = words.shape
    if fmt == "e4m3":
        vals = np.ascontiguousarray(words).view(ml_dtypes.float8_e4m3fn).astype(np.float64)
    else:
        nib = np.empty((g, p, n, 4), np.uint8)
        nib[..., 0::2] = words & 0xF
        nib[..., 1::2] = words >> 4
        vals = E2M1[nib]
    vals = vals * np.repeat(np.exp2(scales.astype(np.float64) - 127.0), 8, axis=1)[..., None]
    return vals.transpose(0, 1, 3, 2).reshape(g * 512, n)
def pack4(w):
    words, scales = pack_weight(w, "e2m1")
    return words.reshape(words.shape[0], 128, -1), scales


def unpack4(words, scales):
    return unpack_weight(words.reshape(words.shape[0], 128, -1, 2), scales, "e2m1")


L, B, N, J, S = 1024, 1024, 1024, 512, 1024


def setup_inputs():
    s = mx_kscale(L)
    t = mx_kscale(N)
    u = mx_kscale(N)
    w = mx_kscale(J)
    c = N ** 0.25
    path = np.random.standard_normal((L, B)) * s[:, None]
    zr = np.random.standard_normal((L, N)) / np.sqrt(L) / s[:, None] * t
    zx = np.random.standard_normal((L, N)) / np.sqrt(L) / c / s[:, None] * u
    path_words, path_scales = pack4(path)
    zr_words, zr_scales = pack4(zr)
    zx_words, zx_scales = pack4(zx)
    return {"path_words": path_words, "path_scales": path_scales,
            "zr_words": zr_words, "zr_scales": zr_scales,
            "zx_words": zx_words, "zx_scales": zx_scales,
            "inj": bf(np.random.standard_normal((N, S)) / np.sqrt(N) / t[:, None]),
            "droop": bf(np.random.standard_normal((N, J)) / np.sqrt(J) / c * w / u[:, None]),
            "dev": bf(np.random.standard_normal((J, S)) / w[:, None]),
            "lo": bf(-np.random.uniform(0.4, 1.2, N) / c / u),
            "hi": bf(np.random.uniform(0.5, 1.5, N) / c / u)}


def reference(path_words, path_scales, zr_words, zr_scales, zx_words, zx_scales, inj, droop, dev, lo, hi):
    a = unpack4(path_words, path_scales)
    r = a.T @ unpack4(zr_words, zr_scales)
    x = a.T @ unpack4(zx_words, zx_scales)
    d = mxq(f64(droop), 1, "e4m3") @ mxq(f64(dev), 0, "e4m3")
    d = np.maximum(np.minimum(d, f64(hi)[:, None]), f64(lo)[:, None])
    active = mxq(r, 1, "e4m3") @ mxq(f64(inj), 0, "e4m3")
    reactive = mxq(x, 1, "e4m3") @ mxq(d, 0, "e4m3")
    return active + reactive

@@ -1,0 +1,366 @@
+from contextlib import ExitStack
+
+import concourse.mybir as mybir
+from concourse.masks import make_identity
+
+L, B, N, J, S = 1024, 1024, 1024, 512, 1024
+FLOPS = 2 * (2 * L * B * N + N * J * S + 2 * B * N * S)
+
+F32 = mybir.dt.float32
+BF16 = mybir.dt.bfloat16
+I32 = mybir.dt.int32
+U32 = mybir.dt.uint32
+U8 = mybir.dt.uint8
+FP8X4 = mybir.dt.float8_e4m3fn_x4
+FP4X4 = mybir.dt.float4_e2m1fn_x4
+ALU = mybir.AluOpType
+
+P = 128
+HALF = 512
+WIDE = ()
+PAIR_BUFS = 4
+
+
+def tile_lindistflow_droop_voltages_s12_kernel(
+    tc, path_words, path_scales, zr_words, zr_scales, zx_words, zx_scales, inj, droop, dev, lo, hi, out
+):
+    nc = tc.nc
+    with ExitStack() as ctx:
+        keep = ctx.enter_context(tc.tile_pool(name="keep", bufs=1))
+        work = ctx.enter_context(tc.tile_pool(name="work", bufs=1))
+        psum = ctx.enter_context(tc.psum_pool(name="psum", bufs=8))
+        ctx.enter_context(tc.manual_schedule())
+
+        def kept(name, shape, dtype):
+            return keep.tile(shape, dtype, name=name, align_bytes=64)
+
+        def new_bank():
+            return psum.tile([P, HALF], F32, name="bank", tag="bank")
+
+        a_words = [kept("a_words%d" % c, [P, 2, w], U8) for c, w in enumerate((512, 512, 1024))]
+        a_plane = kept("a_plane", [P, 2, B], U8)
+        zr_raw = [kept("zr_raw%d" % g, [P, 2, 1024], U8) for g in range(2)]
+        zx_raw = kept("zx_raw", [P, 2, 2048], U8)
+        z_raw = [[zr_raw[0][:], zr_raw[1][:]], [zx_raw[:, :, 0:1024], zx_raw[:, :, 1024:2048]]]
+        z_raw_plane = [kept("z_raw_plane%d" % m, [P, 2, N], U8) for m in range(2)]
+        z_words = [[kept("z_words%d%d" % (m, g), [P, 2, 4, 256], U8) for g in range(2)] for m in range(2)]
+        z_plane = [[kept("z_plane%d%d" % (m, g), [P, 2, 4, 128], U8) for g in range(2)] for m in range(2)]
+        droop_raw = [kept("droop_raw%d" % i, [P, 2, J], BF16) for i in range(4)]
+        droop_t = [kept("droop_t%d" % g, [P, HALF * 4], BF16) for g in range(2)]
+        droop_codes = [kept("droop_codes%d" % g, [P, HALF], U32) for g in range(2)]
+        droop_plane = [kept("droop_plane%d" % g, [P, HALF], U8) for g in range(2)]
+        dev_raw = [kept("dev_raw%d" % h, [P, 4, HALF], BF16) for h in range(2)]
+        dev_codes = [kept("dev_codes%d" % h, [P, HALF], U32) for h in range(2)]
+        dev_plane = [kept("dev_plane%d" % h, [P, HALF], U8) for h in range(2)]
+        mv_raw = [[[kept("mv_raw%d%d%d" % (m, g, h), [P, 4, HALF], BF16) for h in range(2)] for g in range(2)] for m in range(2)]
+        mv_codes = [[[kept("mv_codes%d%d%d" % (m, g, h), [P, HALF], U32) for h in range(2)] for g in range(2)] for m in range(2)]
+        mv_plane = [[[kept("mv_plane%d%d%d" % (m, g, h), [P, HALF], U8) for h in range(2)] for g in range(2)] for m in range(2)]
+        st_bf = [[kept("st_bf%d%d" % (m, c), [P, 2, 256, 4], BF16) for c in range(4)] for m in range(2)]
+        st_codes = [[kept("st_codes%d%d" % (m, c), [P, 2 * 256], U32) for c in range(4)] for m in range(2)]
+        st_plane = [[kept("st_plane%d%d" % (m, c), [P, 2 * 256], U8) for c in range(4)] for m in range(2)]
+        ident_bf = kept("ident_bf", [P, P], BF16)
+        ident = kept("ident", [P, P], F32)
+        limit_rows = kept("limit_rows", [P, P], BF16)
+        limits = kept("limits", [P, 16], F32)
+
+        def load_words(dst, src):
+            nc.sync.dma_start(out=dst[:].bitcast(I32), in_=src.rearrange("g p n -> p g n").bitcast(I32))
+
+        def load_plane(queue, dst, src, q):
+            queue.dma_start(
+                out=dst[32 * q : 32 * q + 4].bitcast(I32),
+                in_=src[:, 4 * q : 4 * q + 4, :].rearrange("g r n -> r g n").bitcast(I32),
+            )
+
+        inj_rows = inj.rearrange("(g q t r) s -> g t q r s", g=2, t=4, r=8)
+
+        def load_inj(g, h):
+            for t in range(4):
+                nc.sync.dma_start(out=mv_raw[0][g][h][:, t, :], in_=inj_rows[g, t, :, :, h * HALF : (h + 1) * HALF])
+
+        def load_dev(h):
+            nc.sync.dma_start(out=dev_raw[h][:], in_=dev.rearrange("(p t) s -> p t s", t=4)[:, :, h * HALF : (h + 1) * HALF])
+
+        def load_limits():
+            for i, vec in enumerate((lo, hi)):
+                rows = vec.rearrange("(g q t r) -> g t q r", g=2, t=4, r=8)
+                for g in range(2):
+                    first = 8 * i + 4 * g
+                    nc.gpsimd.dma_start(out=limit_rows[first : first + 4, :].rearrange("t (q r) -> t q r", r=8), in_=rows[g])
+
+        def permute(m, g):
+            src = z_raw[m][g].bitcast(I32).rearrange("p l (q t w) -> p l t q w", t=4, w=4)
+            nc.vector.tensor_copy(out=z_words[m][g][:].bitcast(I32).rearrange("p l t (q w) -> p l t q w", w=4), in_=src)
+
+        def permute_plane(m, g):
+            src = z_raw_plane[m][:, :, g * HALF : (g + 1) * HALF].bitcast(I32).rearrange("p l (q t w) -> p l t q w", t=4, w=2)
+            nc.vector.tensor_copy(out=z_plane[m][g][:].bitcast(I32).rearrange("p l t (q w) -> p l t q w", w=2), in_=src)
+
+        def a_cols(b0, width):
+            c = min(b0 // 256, 2)
+            first = 2 * (b0 - 256 * c)
+            return [a_words[c][:, l, first : first + 2 * width].bitcast(FP4X4) for l in range(2)]
+
+        def rx_passes(dst, m, g, t, b0, width):
+            cols = a_cols(b0, width)
+            for l in range(2):
+                nc.tensor.matmul_mx(
+                    out=dst,
+                    lhsT=z_words[m][g][:, l, t, :].bitcast(FP4X4),
+                    lhsT_scale=z_plane[m][g][:, l, t, :],
+                    rhs=cols[l],
+                    rhs_scale=a_plane[:, l, b0 : b0 + width],
+                    start=(l == 0),
+                    stop=(l == 1),
+                )
+
+        pairs = {}
+
+        def rx_bank(m, c, g, i):
+            bank = new_bank()
+            if (m, c) in WIDE:
+                if (m, c) not in pairs:
+                    pairs.setdefault((m, c), work.tile([P, 2, 2, 256, 2], BF16, name="pair", tag="pair", bufs=PAIR_BUFS, align_bytes=64))
+                for e in range(2):
+                    rx_passes(bank[:, e * 256 : (e + 1) * 256], m, g, 2 * i + e, 256 * c, 256)
+                nc.scalar.copy(out=pairs[(m, c)][:, g, i], in_=bank[:].rearrange("p (e n) -> p n e", e=2))
+            else:
+                for t in range(4):
+                    rx_passes(bank[:, t * P : (t + 1) * P], m, g, t, 256 * c + P * i, P)
+                nc.scalar.copy(out=st_bf[m][c][:, g, i * P : (i + 1) * P], in_=bank[:].rearrange("p (t n) -> p n t", t=4))
+
+        def rx_unit(m, c):
+            for g in range(2):
+                for i in range(2):
+                    rx_bank(m, c, g, i)
+
+        def rx_join(m, c):
+            if (m, c) in WIDE:
+                nc.vector.tensor_copy(
+                    out=st_bf[m][c][:].bitcast(F32),
+                    in_=pairs[(m, c)][:].rearrange("p g u n e -> p g u (n e)").bitcast(F32).rearrange("p g u n -> p g n u"),
+                )
+
+        def rx_quant(m, c):
+            nc.vector.quantize_mx(
+                out=st_codes[m][c][:].bitcast(FP8X4),
+                scales=st_plane[m][c][:],
+                in_=st_bf[m][c][:].rearrange("p g n t -> p (g n t)"),
+            )
+
+        def droop_bank(i):
+            bank = new_bank()
+            for rr in range(2):
+                words = droop_raw[i][:, rr, :].bitcast(F32)
+                for u in range(2):
+                    c = (2 * rr + u) * P
+                    nc.tensor.transpose(bank[:, c : c + P], words[:, u : 256 : 2], ident[:])
+            turned = bank[:].rearrange("p (r u g q t) -> p g t q r u", r=2, u=2, g=2, t=4)
+            for g in range(2):
+                dst = droop_t[g][:].bitcast(F32).rearrange("p (t q r u) -> p t q r u", t=4, r=8, u=2)[:, :, :, 2 * i : 2 * i + 2, :]
+                nc.scalar.copy(out=dst, in_=turned[:, g])
+
+        def droop_quant(g):
+            nc.vector.quantize_mx(out=droop_codes[g][:].bitcast(FP8X4), scales=droop_plane[g][:], in_=droop_t[g][:])
+
+        def limits_step():
+            bank = new_bank()
+            turned = bank[:].bitcast(BF16)
+            nc.tensor.transpose(turned[:, 0:P], limit_rows[:], ident_bf[:])
+            nc.vector.tensor_copy(out=limits[:], in_=turned[:, 0:16])
+
+        def interleave(raw, copy, parts=1):
+            grouped = work.tile([P, HALF, 4], BF16, name="grouped", tag="grouped", bufs=4, align_bytes=64)
+            copy(
+                out=grouped[:].rearrange("p (c i) t -> p c t i", i=4),
+                in_=raw[:].rearrange("p t (c i) -> p c t i", i=4),
+            )
+            return grouped
+
+        def quant(grouped, codes, plane):
+            nc.vector.quantize_mx(out=codes[:].bitcast(FP8X4), scales=plane[:], in_=grouped[:].rearrange("p c t -> p (c t)"))
+
+        def mv_il(m, g, h, copy):
+            return interleave(mv_raw[m][g][h], copy)
+
+        def mv_q(grouped, m, g, h):
+            quant(grouped, mv_codes[m][g][h], mv_plane[m][g][h])
+
+        def d_bank(j, h):
+            bank = new_bank()
+            g, t = divmod(j, 4)
+            nc.tensor.matmul_mx(
+                out=bank[:],
+                lhsT=droop_codes[g][:, t * P : (t + 1) * P].bitcast(FP8X4),
+                lhsT_scale=droop_plane[g][:, t * P : (t + 1) * P],
+                rhs=dev_codes[h][:].bitcast(FP8X4),
+                rhs_scale=dev_plane[h][:],
+                start=True,
+                stop=True,
+            )
+            nc.vector.tensor_scalar(
+                out=mv_raw[1][g][h][:, t, :],
+                in0=bank[:],
+                scalar1=limits[:, 8 + j : 9 + j],
+                scalar2=limits[:, j : j + 1],
+                op0=ALU.min,
+                op1=ALU.max,
+            )
+
+        def out_pass(dst, b, s0, width, m, g):
+            c, i = divmod(b, 2)
+            h, first = divmod(s0, HALF)
+            cols = slice(g * 256 + i * P, g * 256 + (i + 1) * P)
+            nc.tensor.matmul_mx(
+                out=dst,
+                lhsT=st_codes[m][c][:, cols].bitcast(FP8X4),
+                lhsT_scale=st_plane[m][c][:, cols],
+                rhs=mv_codes[m][g][h][:, first : first + width].bitcast(FP8X4),
+                rhs_scale=mv_plane[m][g][h][:, first : first + width],
+                start=(m == 0 and g == 0),
+                stop=(m == 1 and g == 1),
+            )
+
+        def out_store(bank, b, s0, width, copy, queue):
+            res = work.tile([P, HALF], F32, name="res", tag="res", bufs=6)
+            copy(out=res[:, 0:width], in_=bank[:, 0:width])
+            queue.dma_start(out=out[b * P : (b + 1) * P, s0 : s0 + width], in_=res[:, 0:width])
+
+        def out_bank(b, s0, width, copy, queue):
+            bank = new_bank()
+            for m in range(2):
+                for g in range(2):
+                    out_pass(bank[:, 0:width], b, s0, width, m, g)
+            out_store(bank, b, s0, width, copy, queue)
+
+        vcopy = nc.vector.tensor_copy
+        scopy = nc.scalar.copy
+
+        nc.gpsimd.memset(a_plane[:].rearrange("p g n -> p (g n)").bitcast(I32), 0)
+        nc.vector.memset(z_raw_plane[0][:].rearrange("p g n -> p (g n)").bitcast(I32), 0)
+        nc.vector.memset(z_raw_plane[1][:].rearrange("p g n -> p (g n)").bitcast(I32), 0)
+        nc.vector.memset(limit_rows[:], 0.0)
+        make_identity(nc, ident_bf[:])
+        nc.scalar.copy(out=ident[:], in_=ident_bf[:])
+        for q in (0, 2, 1, 3):
+            load_plane(nc.gpsimd, z_raw_plane[1], zx_scales, q)
+        load_limits()
+
+        load_words(a_words[0], path_words[:, :, 0:512])
+        load_words(zr_raw[0], zr_words[:, :, 0:1024])
+        for q in (0, 2, 1, 3):
+            load_plane(nc.sync, z_raw_plane[0], zr_scales, q)
+        for q in (0, 2, 1, 3):
+            load_plane(nc.sync, a_plane, path_scales, q)
+        load_words(zr_raw[1], zr_words[:, :, 1024:2048])
+        load_words(a_words[1], path_words[:, :, 512:1024])
+        load_dev(0)
+        load_inj(0, 0)
+        droop_rows = droop.rearrange("(p a) k -> p a k", a=8)
+        for i in range(4):
+            nc.sync.dma_start(out=droop_raw[i][:], in_=droop_rows[:, 2 * i : 2 * i + 2, :])
+        load_words(a_words[2], path_words[:, :, 1024:2048])
+        load_inj(1, 0)
+        load_words(zx_raw, zx_words)
+        load_dev(1)
+        load_inj(0, 1)
+        load_inj(1, 1)
+
+        held = {}
+
+        def il(key, raw, copy, part=None):
+            if key not in held:
+                held.setdefault(key, work.tile([P, HALF, 4], BF16, name="grouped", tag="grouped", bufs=5, align_bytes=64))
+            cols = slice(0, HALF) if part is None else slice(part * 256, (part + 1) * 256)
+            copy(
+                out=held[key][:, cols].rearrange("p (c i) t -> p c t i", i=4),
+                in_=raw[:, :, cols].rearrange("p t (c i) -> p c t i", i=4),
+            )
+
+        def il_mv(m, g, h, copy=vcopy, part=None):
+            il((m, g, h), mv_raw[m][g][h], copy, part)
+
+        def q_mv(m, g, h):
+            mv_q(held[(m, g, h)], m, g, h)
+
+        def il_dev(h):
+            il(h, dev_raw[h], vcopy)
+
+        def q_dev(h):
+            quant(held[h], dev_codes[h], dev_plane[h])
+
+        permute(0, 0)
+        permute_plane(0, 0)
+        permute_plane(0, 1)
+        permute(0, 1)
+        rx_unit(0, 0)
+        il_dev(0)
+        permute_plane(1, 0)
+        q_dev(0)
+        il_mv(0, 0, 0)
+        rx_join(0, 0)
+        q_mv(0, 0, 0)
+        rx_quant(0, 0)
+        rx_unit(0, 1)
+        il_mv(0, 1, 0)
+        permute_plane(1, 1)
+        q_mv(0, 1, 0)
+        for i in range(4):
+            droop_bank(i)
+        limits_step()
+        permute(1, 0)
+        permute(1, 1)
+        droop_quant(0)
+        droop_quant(1)
+        rx_unit(0, 2)
+        vjobs = [
+            [lambda: rx_join(0, 1)],
+            [lambda: rx_quant(0, 1), lambda: il_dev(1)],
+            [lambda: q_dev(1), lambda: rx_join(1, 0)],
+            [lambda: rx_quant(1, 0)],
+            [lambda: il_mv(1, 0, 0)],
+            [lambda: q_mv(1, 0, 0), lambda: rx_join(1, 1)],
+            [lambda: rx_quant(1, 1)],
+            [lambda: rx_join(0, 2)],
+        ]
+        for j in range(8):
+            m, c = ((1, 0), (1, 1), (0, 3), (1, 2))[j // 2]
+            d_bank(j, 0)
+            rx_bank(m, c, j % 2, 0)
+            rx_bank(m, c, j % 2, 1)
+            for job in vjobs[j]:
+                job()
+            if j % 2 == 1:
+                il_mv(0, j // 4, 1, scopy, (j // 2) % 2)
+        il_mv(1, 1, 0)
+        rx_quant(0, 2)
+        q_mv(1, 1, 0)
+        for j in range(4):
+            d_bank(j, 1)
+            rx_bank(1, 3, j // 2, j % 2)
+        rx_join(1, 2)
+        q_mv(0, 0, 1)
+        rx_quant(1, 2)
+        for b in range(4):
+            d_bank(4 + b, 1)
+            out_bank(b, 0, HALF, scopy, nc.sync)
+            if b == 0:
+                rx_join(0, 3)
+            if b == 1:
+                rx_join(1, 3)
+            if b == 2:
+                rx_quant(0, 3)
+            if b == 3:
+                rx_quant(1, 3)
+
+        il_mv(1, 0, 1)
+        q_mv(0, 1, 1)
+        q_mv(1, 0, 1)
+        il_mv(1, 1, 1)
+        for b in range(4, 8):
+            out_bank(b, 0, HALF, scopy, nc.sync)
+        q_mv(1, 1, 1)
+        for b in range(7):
+            out_bank(b, HALF, HALF, scopy if b % 2 == 0 else vcopy, nc.sync)
+        out_bank(7, HALF, 256, vcopy, nc.sync)
+        out_bank(7, HALF + 256, 256, scopy, nc.scalar)

@@ -17,7 +17,7 @@ ALU = mybir.AluOpType
 
 P = 128
 HALF = 512
-WIDE = ()
+WIDE = ((0,0),(0,1),(1,0),(1,1),(0,2),(1,2),(0,3),(1,3))
 PAIR_BUFS = 4
 
 
@@ -239,12 +239,10 @@ def tile_lindistflow_droop_voltages_s12_kernel(
         nc.gpsimd.memset(a_plane[:].rearrange("p g n -> p (g n)").bitcast(I32), 0)
         nc.vector.memset(z_raw_plane[0][:].rearrange("p g n -> p (g n)").bitcast(I32), 0)
         nc.vector.memset(z_raw_plane[1][:].rearrange("p g n -> p (g n)").bitcast(I32), 0)
-        nc.vector.memset(limit_rows[:], 0.0)
         make_identity(nc, ident_bf[:])
-        nc.scalar.copy(out=ident[:], in_=ident_bf[:])
-        for q in (0, 2, 1, 3):
-            load_plane(nc.gpsimd, z_raw_plane[1], zx_scales, q)
+        nc.gpsimd.memset(limit_rows[:], 0.0)
         load_limits()
+        nc.scalar.copy(out=ident[:], in_=ident_bf[:])
 
         load_words(a_words[0], path_words[:, :, 0:512])
         load_words(zr_raw[0], zr_words[:, :, 0:1024])
@@ -252,6 +250,8 @@ def tile_lindistflow_droop_voltages_s12_kernel(
             load_plane(nc.sync, z_raw_plane[0], zr_scales, q)
         for q in (0, 2, 1, 3):
             load_plane(nc.sync, a_plane, path_scales, q)
+        for q in (0, 2, 1, 3):
+            load_plane(nc.sync, z_raw_plane[1], zx_scales, q)
         load_words(zr_raw[1], zr_words[:, :, 1024:2048])
         load_words(a_words[1], path_words[:, :, 512:1024])
         load_dev(0)
@@ -308,10 +308,10 @@ def tile_lindistflow_droop_voltages_s12_kernel(
         for i in range(4):
             droop_bank(i)
         limits_step()
-        permute(1, 0)
-        permute(1, 1)
         droop_quant(0)
+        permute(1, 0)
         droop_quant(1)
+        permute(1, 1)
         rx_unit(0, 2)
         vjobs = [
             [lambda: rx_join(0, 1)],
@@ -336,8 +336,8 @@ def tile_lindistflow_droop_voltages_s12_kernel(
         rx_quant(0, 2)
         q_mv(1, 1, 0)
         for j in range(4):
-            d_bank(j, 1)
             rx_bank(1, 3, j // 2, j % 2)
+            d_bank(j, 1)
         rx_join(1, 2)
         q_mv(0, 0, 1)
         rx_quant(1, 2)
@@ -352,15 +352,23 @@ def tile_lindistflow_droop_voltages_s12_kernel(
                 rx_quant(0, 3)
             if b == 3:
                 rx_quant(1, 3)
+            if b in (1, 2):
+                il_mv(1, 0, 1, scopy, b - 1)
 
-        il_mv(1, 0, 1)
         q_mv(0, 1, 1)
         q_mv(1, 0, 1)
         il_mv(1, 1, 1)
         for b in range(4, 8):
             out_bank(b, 0, HALF, scopy, nc.sync)
         q_mv(1, 1, 1)
-        for b in range(7):
+        group = [new_bank(), new_bank(), new_bank()]
+        for m in range(2):
+            for g in range(2):
+                for b in range(3):
+                    out_pass(group[b][:], b, HALF, HALF, m, g)
+        for b in range(3):
+            out_store(group[b], b, HALF, HALF, scopy if b % 2 == 0 else vcopy, nc.sync)
+        for b in range(3, 7):
             out_bank(b, HALF, HALF, scopy if b % 2 == 0 else vcopy, nc.sync)
         out_bank(7, HALF, 256, vcopy, nc.sync)
         out_bank(7, HALF + 256, 256, scopy, nc.scalar)

@@ -18,7 +18,7 @@ ALU = mybir.AluOpType
 P = 128
 HALF = 512
 WIDE = ((0,0),(0,1),(1,0),(1,1),(0,2),(1,2),(0,3),(1,3))
-PAIR_BUFS = 4
+PAIR_BUFS = 6
 
 
 def tile_lindistflow_droop_voltages_s12_kernel(
@@ -250,18 +250,18 @@ def tile_lindistflow_droop_voltages_s12_kernel(
             load_plane(nc.sync, z_raw_plane[0], zr_scales, q)
         for q in (0, 2, 1, 3):
             load_plane(nc.sync, a_plane, path_scales, q)
-        for q in (0, 2, 1, 3):
-            load_plane(nc.sync, z_raw_plane[1], zx_scales, q)
         load_words(zr_raw[1], zr_words[:, :, 1024:2048])
-        load_words(a_words[1], path_words[:, :, 512:1024])
         load_dev(0)
-        load_inj(0, 0)
         droop_rows = droop.rearrange("(p a) k -> p a k", a=8)
         for i in range(4):
             nc.sync.dma_start(out=droop_raw[i][:], in_=droop_rows[:, 2 * i : 2 * i + 2, :])
+        load_words(a_words[1], path_words[:, :, 512:1024])
         load_words(a_words[2], path_words[:, :, 1024:2048])
-        load_inj(1, 0)
+        load_inj(0, 0)
+        for q in (0, 2, 1, 3):
+            load_plane(nc.sync, z_raw_plane[1], zx_scales, q)
         load_words(zx_raw, zx_words)
+        load_inj(1, 0)
         load_dev(1)
         load_inj(0, 1)
         load_inj(1, 1)
@@ -272,16 +272,24 @@ def tile_lindistflow_droop_voltages_s12_kernel(
             if key not in held:
                 held.setdefault(key, work.tile([P, HALF, 4], BF16, name="grouped", tag="grouped", bufs=5, align_bytes=64))
             cols = slice(0, HALF) if part is None else slice(part * 256, (part + 1) * 256)
-            copy(
-                out=held[key][:, cols].rearrange("p (c i) t -> p c t i", i=4),
-                in_=raw[:, :, cols].rearrange("p t (c i) -> p c t i", i=4),
-            )
+            if copy is vcopy:
+                copy(
+                    out=held[key][:, cols].rearrange("p (c i) t -> p c t i", i=4),
+                    in_=raw[:, :, cols].rearrange("p t (c i) -> p c t i", i=4),
+                )
+            else:
+                copy(out=held[key][:, cols], in_=raw[:, :, cols].rearrange("p t c -> p c t"))
 
         def il_mv(m, g, h, copy=vcopy, part=None):
             il((m, g, h), mv_raw[m][g][h], copy, part)
 
-        def q_mv(m, g, h):
-            mv_q(held[(m, g, h)], m, g, h)
+        def q_mv(m, g, h, part=None):
+            cols = slice(0, HALF) if part is None else slice(part * 256, (part + 1) * 256)
+            nc.vector.quantize_mx(
+                out=mv_codes[m][g][h][:, cols].bitcast(FP8X4),
+                scales=mv_plane[m][g][h][:, cols],
+                in_=held[(m, g, h)][:, cols].rearrange("p c t -> p (c t)"),
+            )
 
         def il_dev(h):
             il(h, dev_raw[h], vcopy)
@@ -289,86 +297,117 @@ def tile_lindistflow_droop_voltages_s12_kernel(
         def q_dev(h):
             quant(held[h], dev_codes[h], dev_plane[h])
 
+        def d_pair(jj, part):
+            bank = new_bank()
+            cols = slice(part * 256, (part + 1) * 256)
+            for e in range(2):
+                g, t = divmod(2 * jj + e, 4)
+                nc.tensor.matmul_mx(
+                    out=bank[:, e * 256 : (e + 1) * 256],
+                    lhsT=droop_codes[g][:, t * P : (t + 1) * P].bitcast(FP8X4),
+                    lhsT_scale=droop_plane[g][:, t * P : (t + 1) * P],
+                    rhs=dev_codes[1][:, cols].bitcast(FP8X4),
+                    rhs_scale=dev_plane[1][:, cols],
+                    start=True,
+                    stop=True,
+                )
+            for e in range(2):
+                j = 2 * jj + e
+                g, t = divmod(j, 4)
+                nc.vector.tensor_scalar(
+                    out=mv_raw[1][g][1][:, t, cols],
+                    in0=bank[:, e * 256 : (e + 1) * 256],
+                    scalar1=limits[:, 8 + j : 9 + j],
+                    scalar2=limits[:, j : j + 1],
+                    op0=ALU.min,
+                    op1=ALU.max,
+                )
+
+        def out_pair(c, part, copy):
+            bank = new_bank()
+            s0 = HALF + 256 * part
+            for i in range(2):
+                for m in range(2):
+                    for g in range(2):
+                        out_pass(bank[:, i * 256 : (i + 1) * 256], 2 * c + i, s0, 256, m, g)
+            res = work.tile([P, HALF], F32, name="res", tag="res", bufs=6)
+            copy(out=res[:], in_=bank[:])
+            nc.sync.dma_start(
+                out=out[256 * c : 256 * (c + 1), s0 : s0 + 256].rearrange("(i p) s -> p i s", i=2),
+                in_=res[:].rearrange("p (i s) -> p i s", i=2),
+            )
+
         permute(0, 0)
         permute_plane(0, 0)
         permute_plane(0, 1)
         permute(0, 1)
         rx_unit(0, 0)
         il_dev(0)
-        permute_plane(1, 0)
         q_dev(0)
-        il_mv(0, 0, 0)
         rx_join(0, 0)
-        q_mv(0, 0, 0)
         rx_quant(0, 0)
-        rx_unit(0, 1)
-        il_mv(0, 1, 0)
-        permute_plane(1, 1)
-        q_mv(0, 1, 0)
         for i in range(4):
             droop_bank(i)
         limits_step()
         droop_quant(0)
-        permute(1, 0)
         droop_quant(1)
-        permute(1, 1)
-        rx_unit(0, 2)
-        vjobs = [
-            [lambda: rx_join(0, 1)],
-            [lambda: rx_quant(0, 1), lambda: il_dev(1)],
-            [lambda: q_dev(1), lambda: rx_join(1, 0)],
-            [lambda: rx_quant(1, 0)],
-            [lambda: il_mv(1, 0, 0)],
-            [lambda: q_mv(1, 0, 0), lambda: rx_join(1, 1)],
-            [lambda: rx_quant(1, 1)],
-            [lambda: rx_join(0, 2)],
-        ]
+        rx_unit(0, 1)
+        il_mv(0, 0, 0)
+        vjobs = {
+            0: [lambda: q_mv(0, 0, 0)],
+            1: [lambda: rx_join(0, 1)],
+            2: [lambda: rx_quant(0, 1)],
+            3: [lambda: permute(1, 0), lambda: permute_plane(1, 0)],
+            4: [lambda: permute(1, 1), lambda: permute_plane(1, 1)],
+            5: [lambda: il_mv(1, 0, 0)],
+            7: [lambda: q_mv(1, 0, 0)],
+        }
         for j in range(8):
-            m, c = ((1, 0), (1, 1), (0, 3), (1, 2))[j // 2]
             d_bank(j, 0)
-            rx_bank(m, c, j % 2, 0)
-            rx_bank(m, c, j % 2, 1)
-            for job in vjobs[j]:
+            rx_bank(0, 2 + j // 4, (j % 4) // 2, j % 2)
+            for job in vjobs.get(j, ()):
                 job()
-            if j % 2 == 1:
-                il_mv(0, j // 4, 1, scopy, (j // 2) % 2)
+        rx_unit(1, 0)
         il_mv(1, 1, 0)
-        rx_quant(0, 2)
+        il_mv(0, 1, 0)
         q_mv(1, 1, 0)
-        for j in range(4):
-            rx_bank(1, 3, j // 2, j % 2)
-            d_bank(j, 1)
+        q_mv(0, 1, 0)
+        rx_join(1, 0)
+        il_dev(1)
+        rx_quant(1, 0)
+        q_dev(1)
+        rx_unit(1, 1)
+        rx_join(1, 1)
+        rx_join(0, 2)
+        rx_quant(1, 1)
+        rx_quant(0, 2)
+        rx_unit(1, 2)
+        rx_unit(1, 3)
         rx_join(1, 2)
-        q_mv(0, 0, 1)
+        rx_join(0, 3)
         rx_quant(1, 2)
-        for b in range(4):
-            d_bank(4 + b, 1)
+        vjobs = [
+            [lambda: rx_quant(0, 3)],
+            [lambda: rx_join(1, 3)],
+            [],
+            [lambda: rx_quant(1, 3), lambda: il_mv(1, 0, 1, vcopy, 0)],
+            [lambda: il_mv(1, 1, 1, vcopy, 0), lambda: q_mv(0, 0, 1, 0), lambda: q_mv(1, 0, 1, 0)],
+            [lambda: q_mv(0, 1, 1, 0), lambda: q_mv(1, 1, 1, 0)],
+            [lambda: il_mv(1, 0, 1, vcopy, 1)],
+            [lambda: q_mv(0, 0, 1, 1), lambda: il_mv(1, 1, 1, vcopy, 1), lambda: q_mv(1, 0, 1, 1)],
+        ]
+        for b in range(8):
             out_bank(b, 0, HALF, scopy, nc.sync)
-            if b == 0:
-                rx_join(0, 3)
-            if b == 1:
-                rx_join(1, 3)
-            if b == 2:
-                rx_quant(0, 3)
-            if b == 3:
-                rx_quant(1, 3)
-            if b in (1, 2):
-                il_mv(1, 0, 1, scopy, b - 1)
-
-        q_mv(0, 1, 1)
-        q_mv(1, 0, 1)
-        il_mv(1, 1, 1)
-        for b in range(4, 8):
-            out_bank(b, 0, HALF, scopy, nc.sync)
-        q_mv(1, 1, 1)
-        group = [new_bank(), new_bank(), new_bank()]
-        for m in range(2):
-            for g in range(2):
-                for b in range(3):
-                    out_pass(group[b][:], b, HALF, HALF, m, g)
-        for b in range(3):
-            out_store(group[b], b, HALF, HALF, scopy if b % 2 == 0 else vcopy, nc.sync)
-        for b in range(3, 7):
-            out_bank(b, HALF, HALF, scopy if b % 2 == 0 else vcopy, nc.sync)
-        out_bank(7, HALF, 256, vcopy, nc.sync)
+            d_pair(b % 4, b // 4)
+            if b % 2 == 0:
+                il_mv(0, (b // 2) % 2, 1, scopy, b // 4)
+            for job in vjobs[b]:
+                job()
+        q_mv(0, 1, 1, 1)
+        q_mv(1, 1, 1, 1)
+        for c in range(4):
+            out_pair(c, 0, scopy)
+        for c in range(3):
+            out_pair(c, 1, scopy if c % 2 == 0 else vcopy)
+        out_bank(6, HALF + 256, 256, vcopy, nc.sync)
         out_bank(7, HALF + 256, 256, scopy, nc.scalar)

@@ -60,8 +60,8 @@ def tile_lindistflow_droop_voltages_s12_kernel(
         st_plane = [[kept("st_plane%d%d" % (m, c), [P, 2 * 256], U8) for c in range(4)] for m in range(2)]
         ident_bf = kept("ident_bf", [P, P], BF16)
         ident = kept("ident", [P, P], F32)
-        limit_rows = kept("limit_rows", [P, P], BF16)
-        limits = kept("limits", [P, 16], F32)
+        limit_rows = kept("limit_rows", [P, 2 * P], BF16)
+        limits = kept("limits", [P, 2, 8], F32)
 
         def load_words(dst, src):
             nc.sync.dma_start(out=dst[:].bitcast(I32), in_=src.rearrange("g p n -> p g n").bitcast(I32))
@@ -83,10 +83,10 @@ def tile_lindistflow_droop_voltages_s12_kernel(
 
         def load_limits():
             for i, vec in enumerate((lo, hi)):
-                rows = vec.rearrange("(g q t r) -> g t q r", g=2, t=4, r=8)
-                for g in range(2):
-                    first = 8 * i + 4 * g
-                    nc.gpsimd.dma_start(out=limit_rows[first : first + 4, :].rearrange("t (q r) -> t q r", r=8), in_=rows[g])
+                nc.gpsimd.dma_start(
+                    out=limit_rows[4 * i : 4 * i + 4, :].rearrange("t (q r) -> t q r", r=8),
+                    in_=vec.rearrange("(q t r) -> t q r", t=4, r=8),
+                )
 
         def permute(m, g):
             src = z_raw[m][g].bitcast(I32).rearrange("p l (q t w) -> p l t q w", t=4, w=4)
@@ -148,17 +148,15 @@ def tile_lindistflow_droop_voltages_s12_kernel(
                 in_=st_bf[m][c][:].rearrange("p g n t -> p (g n t)"),
             )
 
-        def droop_bank(i):
+        def droop_bank(g, i):
             bank = new_bank()
-            for rr in range(2):
-                words = droop_raw[i][:, rr, :].bitcast(F32)
+            for a in range(2):
+                words = droop_raw[2 * g + i][:, a, :].bitcast(F32)
                 for u in range(2):
-                    c = (2 * rr + u) * P
+                    c = (2 * a + u) * P
                     nc.tensor.transpose(bank[:, c : c + P], words[:, u : 256 : 2], ident[:])
-            turned = bank[:].rearrange("p (r u g q t) -> p g t q r u", r=2, u=2, g=2, t=4)
-            for g in range(2):
-                dst = droop_t[g][:].bitcast(F32).rearrange("p (t q r u) -> p t q r u", t=4, r=8, u=2)[:, :, :, 2 * i : 2 * i + 2, :]
-                nc.scalar.copy(out=dst, in_=turned[:, g])
+            dst = droop_t[g][:].bitcast(F32).rearrange("p (t q h i w) -> p t q h i w", t=4, h=2, i=2, w=4)[:, :, :, :, i, :]
+            nc.scalar.copy(out=dst, in_=bank[:].rearrange("p (w q t h) -> p t q h w", w=4, t=4, h=2))
 
         def droop_quant(g):
             nc.vector.quantize_mx(out=droop_codes[g][:].bitcast(FP8X4), scales=droop_plane[g][:], in_=droop_t[g][:])
@@ -166,8 +164,9 @@ def tile_lindistflow_droop_voltages_s12_kernel(
         def limits_step():
             bank = new_bank()
             turned = bank[:].bitcast(BF16)
-            nc.tensor.transpose(turned[:, 0:P], limit_rows[:], ident_bf[:])
-            nc.vector.tensor_copy(out=limits[:], in_=turned[:, 0:16])
+            for g in range(2):
+                nc.tensor.transpose(turned[:, g * P : (g + 1) * P], limit_rows[:, g * P : (g + 1) * P], ident_bf[:])
+            nc.vector.tensor_copy(out=limits[:], in_=turned[:, 0 : 2 * P].rearrange("p (g c) -> p g c", g=2)[:, :, 0:8])
 
         def interleave(raw, copy, parts=1):
             grouped = work.tile([P, HALF, 4], BF16, name="grouped", tag="grouped", bufs=4, align_bytes=64)
@@ -201,8 +200,8 @@ def tile_lindistflow_droop_voltages_s12_kernel(
             nc.vector.tensor_scalar(
                 out=mv_raw[1][g][h][:, t, :],
                 in0=bank[:],
-                scalar1=limits[:, 8 + j : 9 + j],
-                scalar2=limits[:, j : j + 1],
+                scalar1=limits[:, g, 4 + t : 5 + t],
+                scalar2=limits[:, g, t : t + 1],
                 op0=ALU.min,
                 op1=ALU.max,
             )
@@ -236,28 +235,33 @@ def tile_lindistflow_droop_voltages_s12_kernel(
         vcopy = nc.vector.tensor_copy
         scopy = nc.scalar.copy
 
-        nc.gpsimd.memset(a_plane[:].rearrange("p g n -> p (g n)").bitcast(I32), 0)
-        nc.vector.memset(z_raw_plane[0][:].rearrange("p g n -> p (g n)").bitcast(I32), 0)
-        nc.vector.memset(z_raw_plane[1][:].rearrange("p g n -> p (g n)").bitcast(I32), 0)
+        nc.vector.memset(limit_rows[:].bitcast(I32), 0)
         make_identity(nc, ident_bf[:])
-        nc.gpsimd.memset(limit_rows[:], 0.0)
         load_limits()
         nc.scalar.copy(out=ident[:], in_=ident_bf[:])
+        warm_bf = kept("warm_bf", [P, HALF], BF16)
+        warm_codes = kept("warm_codes", [P, P], U32)
+        warm_plane = kept("warm_plane", [P, P], U8)
+        nc.vector.memset(warm_bf[:], 1.0)
+        nc.vector.memset(z_raw_plane[0][:].rearrange("p g n -> p (g n)").bitcast(I32), 0)
+        nc.vector.quantize_mx(out=warm_codes[:].bitcast(FP8X4), scales=warm_plane[:], in_=warm_bf[:])
+        nc.vector.memset(a_plane[:].rearrange("p g n -> p (g n)").bitcast(I32), 0)
+        nc.vector.memset(z_raw_plane[1][:].rearrange("p g n -> p (g n)").bitcast(I32), 0)
 
-        load_words(a_words[0], path_words[:, :, 0:512])
+        droop_rows = droop.rearrange("(g p a) k -> g p a k", g=2, a=4)
+        load_dev(0)
+        for i in range(4):
+            nc.sync.dma_start(out=droop_raw[i][:], in_=droop_rows[i // 2, :, 2 * (i % 2) : 2 * (i % 2) + 2, :])
         load_words(zr_raw[0], zr_words[:, :, 0:1024])
+        load_words(a_words[0], path_words[:, :, 0:512])
         for q in (0, 2, 1, 3):
             load_plane(nc.sync, z_raw_plane[0], zr_scales, q)
         for q in (0, 2, 1, 3):
             load_plane(nc.sync, a_plane, path_scales, q)
         load_words(zr_raw[1], zr_words[:, :, 1024:2048])
-        load_dev(0)
-        droop_rows = droop.rearrange("(p a) k -> p a k", a=8)
-        for i in range(4):
-            nc.sync.dma_start(out=droop_raw[i][:], in_=droop_rows[:, 2 * i : 2 * i + 2, :])
         load_words(a_words[1], path_words[:, :, 512:1024])
-        load_words(a_words[2], path_words[:, :, 1024:2048])
         load_inj(0, 0)
+        load_words(a_words[2], path_words[:, :, 1024:2048])
         for q in (0, 2, 1, 3):
             load_plane(nc.sync, z_raw_plane[1], zx_scales, q)
         load_words(zx_raw, zx_words)
@@ -317,8 +321,8 @@ def tile_lindistflow_droop_voltages_s12_kernel(
                 nc.vector.tensor_scalar(
                     out=mv_raw[1][g][1][:, t, cols],
                     in0=bank[:, e * 256 : (e + 1) * 256],
-                    scalar1=limits[:, 8 + j : 9 + j],
-                    scalar2=limits[:, j : j + 1],
+                    scalar1=limits[:, g, 4 + t : 5 + t],
+                    scalar2=limits[:, g, t : t + 1],
                     op0=ALU.min,
                     op1=ALU.max,
                 )
@@ -337,74 +341,86 @@ def tile_lindistflow_droop_voltages_s12_kernel(
                 in_=res[:].rearrange("p (i s) -> p i s", i=2),
             )
 
-        permute(0, 0)
-        permute_plane(0, 0)
-        permute_plane(0, 1)
-        permute(0, 1)
-        rx_unit(0, 0)
+        warm_bank = new_bank()
+        for i in range(14):
+            nc.tensor.matmul_mx(
+                out=warm_bank[:, 0:P],
+                lhsT=warm_codes[:].bitcast(FP8X4),
+                lhsT_scale=warm_plane[:],
+                rhs=warm_codes[:].bitcast(FP8X4),
+                rhs_scale=warm_plane[:],
+                start=True,
+                stop=True,
+            )
         il_dev(0)
+        droop_bank(0, 0)
+        droop_bank(0, 1)
         q_dev(0)
-        rx_join(0, 0)
-        rx_quant(0, 0)
-        for i in range(4):
-            droop_bank(i)
-        limits_step()
         droop_quant(0)
+        droop_bank(1, 0)
+        droop_bank(1, 1)
+        limits_step()
+        permute(0, 0)
         droop_quant(1)
-        rx_unit(0, 1)
-        il_mv(0, 0, 0)
-        vjobs = {
-            0: [lambda: q_mv(0, 0, 0)],
-            1: [lambda: rx_join(0, 1)],
-            2: [lambda: rx_quant(0, 1)],
-            3: [lambda: permute(1, 0), lambda: permute_plane(1, 0)],
-            4: [lambda: permute(1, 1), lambda: permute_plane(1, 1)],
-            5: [lambda: il_mv(1, 0, 0)],
-            7: [lambda: q_mv(1, 0, 0)],
-        }
+        permute_plane(0, 0)
         for j in range(8):
             d_bank(j, 0)
-            rx_bank(0, 2 + j // 4, (j % 4) // 2, j % 2)
-            for job in vjobs.get(j, ()):
-                job()
-        rx_unit(1, 0)
+            if j == 2:
+                permute(0, 1)
+                permute_plane(0, 1)
+        rx_unit(0, 0)
+        rx_unit(0, 1)
+        il_mv(1, 0, 0)
         il_mv(1, 1, 0)
-        il_mv(0, 1, 0)
+        q_mv(1, 0, 0)
         q_mv(1, 1, 0)
-        q_mv(0, 1, 0)
-        rx_join(1, 0)
+        rx_unit(0, 2)
+        permute(1, 0)
+        permute_plane(1, 0)
+        il_mv(0, 0, 0)
+        permute(1, 1)
+        permute_plane(1, 1)
+        q_mv(0, 0, 0)
+        rx_unit(0, 3)
+        il_mv(0, 1, 0, scopy, 0)
+        rx_join(0, 0)
         il_dev(1)
-        rx_quant(1, 0)
+        rx_quant(0, 0)
         q_dev(1)
+        rx_unit(1, 0)
+        il_mv(0, 1, 0, scopy, 1)
+        rx_join(0, 1)
+        rx_join(1, 0)
+        rx_quant(0, 1)
+        rx_quant(1, 0)
         rx_unit(1, 1)
-        rx_join(1, 1)
+        q_mv(0, 1, 0)
         rx_join(0, 2)
-        rx_quant(1, 1)
+        rx_join(1, 1)
         rx_quant(0, 2)
+        rx_quant(1, 1)
         rx_unit(1, 2)
-        rx_unit(1, 3)
-        rx_join(1, 2)
-        rx_join(0, 3)
-        rx_quant(1, 2)
+        for i in range(4):
+            rx_bank(1, 3, i // 2, i % 2)
+            d_pair(i, 0)
         vjobs = [
-            [lambda: rx_quant(0, 3)],
-            [lambda: rx_join(1, 3)],
-            [],
-            [lambda: rx_quant(1, 3), lambda: il_mv(1, 0, 1, vcopy, 0)],
-            [lambda: il_mv(1, 1, 1, vcopy, 0), lambda: q_mv(0, 0, 1, 0), lambda: q_mv(1, 0, 1, 0)],
-            [lambda: q_mv(0, 1, 1, 0), lambda: q_mv(1, 1, 1, 0)],
-            [lambda: il_mv(1, 0, 1, vcopy, 1)],
-            [lambda: q_mv(0, 0, 1, 1), lambda: il_mv(1, 1, 1, vcopy, 1), lambda: q_mv(1, 0, 1, 1)],
+            [lambda: rx_join(1, 2)],
+            [lambda: rx_join(0, 3), lambda: rx_quant(1, 2)],
+            [lambda: rx_join(1, 3), lambda: rx_quant(0, 3)],
+            [lambda: rx_quant(1, 3)],
+            [lambda: il_mv(1, 0, 1, vcopy, 0), lambda: il_mv(1, 1, 1, vcopy, 0), lambda: q_mv(1, 0, 1, 0), lambda: q_mv(1, 1, 1, 0)],
+            [lambda: q_mv(0, 0, 1, 0), lambda: q_mv(0, 1, 1, 0)],
+            [lambda: il_mv(1, 0, 1, vcopy, 1), lambda: il_mv(1, 1, 1, vcopy, 1), lambda: q_mv(1, 0, 1, 1), lambda: q_mv(1, 1, 1, 1)],
+            [lambda: q_mv(0, 0, 1, 1), lambda: q_mv(0, 1, 1, 1)],
         ]
         for b in range(8):
             out_bank(b, 0, HALF, scopy, nc.sync)
-            d_pair(b % 4, b // 4)
+            if b < 4:
+                d_pair(b, 1)
             if b % 2 == 0:
                 il_mv(0, (b // 2) % 2, 1, scopy, b // 4)
             for job in vjobs[b]:
                 job()
-        q_mv(0, 1, 1, 1)
-        q_mv(1, 1, 1, 1)
         for c in range(4):
             out_pair(c, 0, scopy)
         for c in range(3):

@@ -239,12 +239,7 @@ def tile_lindistflow_droop_voltages_s12_kernel(
         make_identity(nc, ident_bf[:])
         load_limits()
         nc.scalar.copy(out=ident[:], in_=ident_bf[:])
-        warm_bf = kept("warm_bf", [P, HALF], BF16)
-        warm_codes = kept("warm_codes", [P, P], U32)
-        warm_plane = kept("warm_plane", [P, P], U8)
-        nc.vector.memset(warm_bf[:], 1.0)
         nc.vector.memset(z_raw_plane[0][:].rearrange("p g n -> p (g n)").bitcast(I32), 0)
-        nc.vector.quantize_mx(out=warm_codes[:].bitcast(FP8X4), scales=warm_plane[:], in_=warm_bf[:])
         nc.vector.memset(a_plane[:].rearrange("p g n -> p (g n)").bitcast(I32), 0)
         nc.vector.memset(z_raw_plane[1][:].rearrange("p g n -> p (g n)").bitcast(I32), 0)
 
@@ -260,11 +255,11 @@ def tile_lindistflow_droop_voltages_s12_kernel(
             load_plane(nc.sync, a_plane, path_scales, q)
         load_words(zr_raw[1], zr_words[:, :, 1024:2048])
         load_words(a_words[1], path_words[:, :, 512:1024])
-        load_inj(0, 0)
-        load_words(a_words[2], path_words[:, :, 1024:2048])
         for q in (0, 2, 1, 3):
             load_plane(nc.sync, z_raw_plane[1], zx_scales, q)
         load_words(zx_raw, zx_words)
+        load_inj(0, 0)
+        load_words(a_words[2], path_words[:, :, 1024:2048])
         load_inj(1, 0)
         load_dev(1)
         load_inj(0, 1)
@@ -341,17 +336,6 @@ def tile_lindistflow_droop_voltages_s12_kernel(
                 in_=res[:].rearrange("p (i s) -> p i s", i=2),
             )
 
-        warm_bank = new_bank()
-        for i in range(14):
-            nc.tensor.matmul_mx(
-                out=warm_bank[:, 0:P],
-                lhsT=warm_codes[:].bitcast(FP8X4),
-                lhsT_scale=warm_plane[:],
-                rhs=warm_codes[:].bitcast(FP8X4),
-                rhs_scale=warm_plane[:],
-                start=True,
-                stop=True,
-            )
         il_dev(0)
         droop_bank(0, 0)
         droop_bank(0, 1)
@@ -370,57 +354,62 @@ def tile_lindistflow_droop_voltages_s12_kernel(
                 permute_plane(0, 1)
         rx_unit(0, 0)
         rx_unit(0, 1)
+        for g in range(2):
+            permute(1, g)
+            permute_plane(1, g)
+        rx_unit(1, 0)
         il_mv(1, 0, 0)
         il_mv(1, 1, 0)
         q_mv(1, 0, 0)
         q_mv(1, 1, 0)
-        rx_unit(0, 2)
-        permute(1, 0)
-        permute_plane(1, 0)
-        il_mv(0, 0, 0)
-        permute(1, 1)
-        permute_plane(1, 1)
-        q_mv(0, 0, 0)
-        rx_unit(0, 3)
-        il_mv(0, 1, 0, scopy, 0)
-        rx_join(0, 0)
-        il_dev(1)
-        rx_quant(0, 0)
-        q_dev(1)
-        rx_unit(1, 0)
-        il_mv(0, 1, 0, scopy, 1)
-        rx_join(0, 1)
-        rx_join(1, 0)
-        rx_quant(0, 1)
-        rx_quant(1, 0)
         rx_unit(1, 1)
+        il_mv(0, 0, 0)
+        il_dev(1)
+        q_mv(0, 0, 0)
+        q_dev(1)
+        rx_unit(0, 2)
+        il_mv(0, 1, 0)
+        rx_join(0, 0)
         q_mv(0, 1, 0)
-        rx_join(0, 2)
-        rx_join(1, 1)
-        rx_quant(0, 2)
-        rx_quant(1, 1)
+        rx_join(1, 0)
+        rx_quant(0, 0)
+        rx_quant(1, 0)
         rx_unit(1, 2)
-        for i in range(4):
-            rx_bank(1, 3, i // 2, i % 2)
-            d_pair(i, 0)
-        vjobs = [
-            [lambda: rx_join(1, 2)],
-            [lambda: rx_join(0, 3), lambda: rx_quant(1, 2)],
-            [lambda: rx_join(1, 3), lambda: rx_quant(0, 3)],
-            [lambda: rx_quant(1, 3)],
-            [lambda: il_mv(1, 0, 1, vcopy, 0), lambda: il_mv(1, 1, 1, vcopy, 0), lambda: q_mv(1, 0, 1, 0), lambda: q_mv(1, 1, 1, 0)],
-            [lambda: q_mv(0, 0, 1, 0), lambda: q_mv(0, 1, 1, 0)],
-            [lambda: il_mv(1, 0, 1, vcopy, 1), lambda: il_mv(1, 1, 1, vcopy, 1), lambda: q_mv(1, 0, 1, 1), lambda: q_mv(1, 1, 1, 1)],
-            [lambda: q_mv(0, 0, 1, 1), lambda: q_mv(0, 1, 1, 1)],
-        ]
-        for b in range(8):
+        for b in range(4):
+            if b < 2:
+                d_pair(2 * b, 0)
+                d_pair(2 * b + 1, 0)
+            rx_bank(b // 2, 3, b % 2, 0)
+            rx_bank(b // 2, 3, b % 2, 1)
             out_bank(b, 0, HALF, scopy, nc.sync)
-            if b < 4:
-                d_pair(b, 1)
-            if b % 2 == 0:
-                il_mv(0, (b // 2) % 2, 1, scopy, b // 4)
-            for job in vjobs[b]:
-                job()
+            if b >= 2:
+                il_mv(0, b - 2, 1, scopy, 0)
+            if b < 2:
+                rx_join(0, 1 + b)
+                rx_join(1, 1 + b)
+                rx_quant(0, 1 + b)
+                rx_quant(1, 1 + b)
+            if b == 2:
+                rx_join(0, 3)
+                for g in range(2):
+                    il_mv(1, g, 1, vcopy, 0)
+                rx_quant(0, 3)
+                for g in range(2):
+                    q_mv(1, g, 1, 0)
+        rx_join(1, 3)
+        q_mv(0, 0, 1, 0)
+        rx_quant(1, 3)
+        q_mv(0, 1, 1, 0)
+        for b in range(4, 8):
+            d_pair(b - 4, 1)
+            out_bank(b, 0, HALF, scopy, nc.sync)
+            if b < 6:
+                il_mv(0, b - 4, 1, scopy, 1)
+        for g in range(2):
+            il_mv(1, g, 1, vcopy, 1)
+        for g in range(2):
+            q_mv(0, g, 1, 1)
+            q_mv(1, g, 1, 1)
         for c in range(4):
             out_pair(c, 0, scopy)
         for c in range(3):

from contextlib import ExitStack

import concourse.mybir as mybir
from concourse.masks import make_identity

L, B, N, J, S = 1024, 1024, 1024, 512, 1024
FLOPS = 2 * (2 * L * B * N + N * J * S + 2 * B * N * S)

F32 = mybir.dt.float32
BF16 = mybir.dt.bfloat16
I32 = mybir.dt.int32
U32 = mybir.dt.uint32
U8 = mybir.dt.uint8
FP8X4 = mybir.dt.float8_e4m3fn_x4
FP4X4 = mybir.dt.float4_e2m1fn_x4
ALU = mybir.AluOpType

P = 128
HALF = 512
WIDE = ((0,0),(0,1),(1,0),(1,1),(0,2),(1,2),(0,3),(1,3))
PAIR_BUFS = 6


def tile_lindistflow_droop_voltages_s12_kernel(
    tc, path_words, path_scales, zr_words, zr_scales, zx_words, zx_scales, inj, droop, dev, lo, hi, out
):
    nc = tc.nc
    with ExitStack() as ctx:
        keep = ctx.enter_context(tc.tile_pool(name="keep", bufs=1))
        work = ctx.enter_context(tc.tile_pool(name="work", bufs=1))
        psum = ctx.enter_context(tc.psum_pool(name="psum", bufs=8))
        ctx.enter_context(tc.manual_schedule())

        def kept(name, shape, dtype):
            return keep.tile(shape, dtype, name=name, align_bytes=64)

        def new_bank():
            return psum.tile([P, HALF], F32, name="bank", tag="bank")

        a_words = [kept("a_words%d" % c, [P, 2, w], U8) for c, w in enumerate((512, 512, 1024))]
        a_plane = kept("a_plane", [P, 2, B], U8)
        zr_raw = [kept("zr_raw%d" % g, [P, 2, 1024], U8) for g in range(2)]
        zx_raw = kept("zx_raw", [P, 2, 2048], U8)
        z_raw = [[zr_raw[0][:], zr_raw[1][:]], [zx_raw[:, :, 0:1024], zx_raw[:, :, 1024:2048]]]
        z_raw_plane = [kept("z_raw_plane%d" % m, [P, 2, N], U8) for m in range(2)]
        z_words = [[kept("z_words%d%d" % (m, g), [P, 2, 4, 256], U8) for g in range(2)] for m in range(2)]
        z_plane = [[kept("z_plane%d%d" % (m, g), [P, 2, 4, 128], U8) for g in range(2)] for m in range(2)]
        droop_raw = [kept("droop_raw%d" % i, [P, 2, J], BF16) for i in range(4)]
        droop_t = [kept("droop_t%d" % g, [P, HALF * 4], BF16) for g in range(2)]
        droop_codes = [kept("droop_codes%d" % g, [P, HALF], U32) for g in range(2)]
        droop_plane = [kept("droop_plane%d" % g, [P, HALF], U8) for g in range(2)]
        dev_raw = [kept("dev_raw%d" % h, [P, 4, HALF], BF16) for h in range(2)]
        dev_codes = [kept("dev_codes%d" % h, [P, HALF], U32) for h in range(2)]
        dev_plane = [kept("dev_plane%d" % h, [P, HALF], U8) for h in range(2)]
        mv_raw = [[[kept("mv_raw%d%d%d" % (m, g, h), [P, 4, HALF], BF16) for h in range(2)] for g in range(2)] for m in range(2)]
        mv_codes = [[[kept("mv_codes%d%d%d" % (m, g, h), [P, HALF], U32) for h in range(2)] for g in range(2)] for m in range(2)]
        mv_plane = [[[kept("mv_plane%d%d%d" % (m, g, h), [P, HALF], U8) for h in range(2)] for g in range(2)] for m in range(2)]
        st_bf = [[kept("st_bf%d%d" % (m, c), [P, 2, 256, 4], BF16) for c in range(4)] for m in range(2)]
        st_codes = [[kept("st_codes%d%d" % (m, c), [P, 2 * 256], U32) for c in range(4)] for m in range(2)]
        st_plane = [[kept("st_plane%d%d" % (m, c), [P, 2 * 256], U8) for c in range(4)] for m in range(2)]
        ident_bf = kept("ident_bf", [P, P], BF16)
        ident = kept("ident", [P, P], F32)
        limit_rows = kept("limit_rows", [P, 2 * P], BF16)
        limits = kept("limits", [P, 2, 8], F32)

        def load_words(dst, src):
            nc.sync.dma_start(out=dst[:].bitcast(I32), in_=src.rearrange("g p n -> p g n").bitcast(I32))

        def load_plane(queue, dst, src, q):
            queue.dma_start(
                out=dst[32 * q : 32 * q + 4].bitcast(I32),
                in_=src[:, 4 * q : 4 * q + 4, :].rearrange("g r n -> r g n").bitcast(I32),
            )

        inj_rows = inj.rearrange("(g q t r) s -> g t q r s", g=2, t=4, r=8)

        def load_inj(g, h):
            for t in range(4):
                nc.sync.dma_start(out=mv_raw[0][g][h][:, t, :], in_=inj_rows[g, t, :, :, h * HALF : (h + 1) * HALF])

        def load_dev(h):
            nc.sync.dma_start(out=dev_raw[h][:], in_=dev.rearrange("(p t) s -> p t s", t=4)[:, :, h * HALF : (h + 1) * HALF])

        def load_limits():
            for i, vec in enumerate((lo, hi)):
                nc.gpsimd.dma_start(
                    out=limit_rows[4 * i : 4 * i + 4, :].rearrange("t (q r) -> t q r", r=8),
                    in_=vec.rearrange("(q t r) -> t q r", t=4, r=8),
                )

        def permute(m, g):
            src = z_raw[m][g].bitcast(I32).rearrange("p l (q t w) -> p l t q w", t=4, w=4)
            nc.vector.tensor_copy(out=z_words[m][g][:].bitcast(I32).rearrange("p l t (q w) -> p l t q w", w=4), in_=src)

        def permute_plane(m, g):
            src = z_raw_plane[m][:, :, g * HALF : (g + 1) * HALF].bitcast(I32).rearrange("p l (q t w) -> p l t q w", t=4, w=2)
            nc.vector.tensor_copy(out=z_plane[m][g][:].bitcast(I32).rearrange("p l t (q w) -> p l t q w", w=2), in_=src)

        def a_cols(b0, width):
            c = min(b0 // 256, 2)
            first = 2 * (b0 - 256 * c)
            return [a_words[c][:, l, first : first + 2 * width].bitcast(FP4X4) for l in range(2)]

        def rx_passes(dst, m, g, t, b0, width):
            cols = a_cols(b0, width)
            for l in range(2):
                nc.tensor.matmul_mx(
                    out=dst,
                    lhsT=z_words[m][g][:, l, t, :].bitcast(FP4X4),
                    lhsT_scale=z_plane[m][g][:, l, t, :],
                    rhs=cols[l],
                    rhs_scale=a_plane[:, l, b0 : b0 + width],
                    start=(l == 0),
                    stop=(l == 1),
                )

        pairs = {}

        def rx_bank(m, c, g, i):
            bank = new_bank()
            if (m, c) in WIDE:
                if (m, c) not in pairs:
                    pairs.setdefault((m, c), work.tile([P, 2, 2, 256, 2], BF16, name="pair", tag="pair", bufs=PAIR_BUFS, align_bytes=64))
                for e in range(2):
                    rx_passes(bank[:, e * 256 : (e + 1) * 256], m, g, 2 * i + e, 256 * c, 256)
                nc.scalar.copy(out=pairs[(m, c)][:, g, i], in_=bank[:].rearrange("p (e n) -> p n e", e=2))
            else:
                for t in range(4):
                    rx_passes(bank[:, t * P : (t + 1) * P], m, g, t, 256 * c + P * i, P)
                nc.scalar.copy(out=st_bf[m][c][:, g, i * P : (i + 1) * P], in_=bank[:].rearrange("p (t n) -> p n t", t=4))

        def rx_unit(m, c):
            for g in range(2):
                for i in range(2):
                    rx_bank(m, c, g, i)

        def rx_join(m, c):
            if (m, c) in WIDE:
                nc.vector.tensor_copy(
                    out=st_bf[m][c][:].bitcast(F32),
                    in_=pairs[(m, c)][:].rearrange("p g u n e -> p g u (n e)").bitcast(F32).rearrange("p g u n -> p g n u"),
                )

        def rx_quant(m, c):
            nc.vector.quantize_mx(
                out=st_codes[m][c][:].bitcast(FP8X4),
                scales=st_plane[m][c][:],
                in_=st_bf[m][c][:].rearrange("p g n t -> p (g n t)"),
            )

        def droop_bank(g, i):
            bank = new_bank()
            for a in range(2):
                words = droop_raw[2 * g + i][:, a, :].bitcast(F32)
                for u in range(2):
                    c = (2 * a + u) * P
                    nc.tensor.transpose(bank[:, c : c + P], words[:, u : 256 : 2], ident[:])
            dst = droop_t[g][:].bitcast(F32).rearrange("p (t q h i w) -> p t q h i w", t=4, h=2, i=2, w=4)[:, :, :, :, i, :]
            nc.scalar.copy(out=dst, in_=bank[:].rearrange("p (w q t h) -> p t q h w", w=4, t=4, h=2))

        def droop_quant(g):
            nc.vector.quantize_mx(out=droop_codes[g][:].bitcast(FP8X4), scales=droop_plane[g][:], in_=droop_t[g][:])

        def limits_step():
            bank = new_bank()
            turned = bank[:].bitcast(BF16)
            for g in range(2):
                nc.tensor.transpose(turned[:, g * P : (g + 1) * P], limit_rows[:, g * P : (g + 1) * P], ident_bf[:])
            nc.vector.tensor_copy(out=limits[:], in_=turned[:, 0 : 2 * P].rearrange("p (g c) -> p g c", g=2)[:, :, 0:8])

        def interleave(raw, copy, parts=1):
            grouped = work.tile([P, HALF, 4], BF16, name="grouped", tag="grouped", bufs=4, align_bytes=64)
            copy(
                out=grouped[:].rearrange("p (c i) t -> p c t i", i=4),
                in_=raw[:].rearrange("p t (c i) -> p c t i", i=4),
            )
            return grouped

        def quant(grouped, codes, plane):
            nc.vector.quantize_mx(out=codes[:].bitcast(FP8X4), scales=plane[:], in_=grouped[:].rearrange("p c t -> p (c t)"))

        def mv_il(m, g, h, copy):
            return interleave(mv_raw[m][g][h], copy)

        def mv_q(grouped, m, g, h):
            quant(grouped, mv_codes[m][g][h], mv_plane[m][g][h])

        def d_bank(j, h):
            bank = new_bank()
            g, t = divmod(j, 4)
            nc.tensor.matmul_mx(
                out=bank[:],
                lhsT=droop_codes[g][:, t * P : (t + 1) * P].bitcast(FP8X4),
                lhsT_scale=droop_plane[g][:, t * P : (t + 1) * P],
                rhs=dev_codes[h][:].bitcast(FP8X4),
                rhs_scale=dev_plane[h][:],
                start=True,
                stop=True,
            )
            nc.vector.tensor_scalar(
                out=mv_raw[1][g][h][:, t, :],
                in0=bank[:],
                scalar1=limits[:, g, 4 + t : 5 + t],
                scalar2=limits[:, g, t : t + 1],
                op0=ALU.min,
                op1=ALU.max,
            )

        def out_pass(dst, b, s0, width, m, g):
            c, i = divmod(b, 2)
            h, first = divmod(s0, HALF)
            cols = slice(g * 256 + i * P, g * 256 + (i + 1) * P)
            nc.tensor.matmul_mx(
                out=dst,
                lhsT=st_codes[m][c][:, cols].bitcast(FP8X4),
                lhsT_scale=st_plane[m][c][:, cols],
                rhs=mv_codes[m][g][h][:, first : first + width].bitcast(FP8X4),
                rhs_scale=mv_plane[m][g][h][:, first : first + width],
                start=(m == 0 and g == 0),
                stop=(m == 1 and g == 1),
            )

        def out_store(bank, b, s0, width, copy, queue):
            res = work.tile([P, HALF], F32, name="res", tag="res", bufs=6)
            copy(out=res[:, 0:width], in_=bank[:, 0:width])
            queue.dma_start(out=out[b * P : (b + 1) * P, s0 : s0 + width], in_=res[:, 0:width])

        def out_bank(b, s0, width, copy, queue):
            bank = new_bank()
            for m in range(2):
                for g in range(2):
                    out_pass(bank[:, 0:width], b, s0, width, m, g)
            out_store(bank, b, s0, width, copy, queue)

        vcopy = nc.vector.tensor_copy
        scopy = nc.scalar.copy

        nc.vector.memset(limit_rows[:].bitcast(I32), 0)
        make_identity(nc, ident_bf[:])
        load_limits()
        nc.scalar.copy(out=ident[:], in_=ident_bf[:])
        nc.vector.memset(z_raw_plane[0][:].rearrange("p g n -> p (g n)").bitcast(I32), 0)
        nc.vector.memset(a_plane[:].rearrange("p g n -> p (g n)").bitcast(I32), 0)
        nc.vector.memset(z_raw_plane[1][:].rearrange("p g n -> p (g n)").bitcast(I32), 0)

        droop_rows = droop.rearrange("(g p a) k -> g p a k", g=2, a=4)
        load_dev(0)
        for i in range(4):
            nc.sync.dma_start(out=droop_raw[i][:], in_=droop_rows[i // 2, :, 2 * (i % 2) : 2 * (i % 2) + 2, :])
        load_words(zr_raw[0], zr_words[:, :, 0:1024])
        load_words(a_words[0], path_words[:, :, 0:512])
        for q in (0, 2, 1, 3):
            load_plane(nc.sync, z_raw_plane[0], zr_scales, q)
        for q in (0, 2, 1, 3):
            load_plane(nc.sync, a_plane, path_scales, q)
        load_words(zr_raw[1], zr_words[:, :, 1024:2048])
        load_words(a_words[1], path_words[:, :, 512:1024])
        for q in (0, 2, 1, 3):
            load_plane(nc.sync, z_raw_plane[1], zx_scales, q)
        load_words(zx_raw, zx_words)
        load_inj(0, 0)
        load_words(a_words[2], path_words[:, :, 1024:2048])
        load_inj(1, 0)
        load_dev(1)
        load_inj(0, 1)
        load_inj(1, 1)

        held = {}

        def il(key, raw, copy, part=None):
            if key not in held:
                held.setdefault(key, work.tile([P, HALF, 4], BF16, name="grouped", tag="grouped", bufs=5, align_bytes=64))
            cols = slice(0, HALF) if part is None else slice(part * 256, (part + 1) * 256)
            if copy is vcopy:
                copy(
                    out=held[key][:, cols].rearrange("p (c i) t -> p c t i", i=4),
                    in_=raw[:, :, cols].rearrange("p t (c i) -> p c t i", i=4),
                )
            else:
                copy(out=held[key][:, cols], in_=raw[:, :, cols].rearrange("p t c -> p c t"))

        def il_mv(m, g, h, copy=vcopy, part=None):
            il((m, g, h), mv_raw[m][g][h], copy, part)

        def q_mv(m, g, h, part=None):
            cols = slice(0, HALF) if part is None else slice(part * 256, (part + 1) * 256)
            nc.vector.quantize_mx(
                out=mv_codes[m][g][h][:, cols].bitcast(FP8X4),
                scales=mv_plane[m][g][h][:, cols],
                in_=held[(m, g, h)][:, cols].rearrange("p c t -> p (c t)"),
            )

        def il_dev(h):
            il(h, dev_raw[h], vcopy)

        def q_dev(h):
            quant(held[h], dev_codes[h], dev_plane[h])

        def d_pair(jj, part):
            bank = new_bank()
            cols = slice(part * 256, (part + 1) * 256)
            for e in range(2):
                g, t = divmod(2 * jj + e, 4)
                nc.tensor.matmul_mx(
                    out=bank[:, e * 256 : (e + 1) * 256],
                    lhsT=droop_codes[g][:, t * P : (t + 1) * P].bitcast(FP8X4),
                    lhsT_scale=droop_plane[g][:, t * P : (t + 1) * P],
                    rhs=dev_codes[1][:, cols].bitcast(FP8X4),
                    rhs_scale=dev_plane[1][:, cols],
                    start=True,
                    stop=True,
                )
            for e in range(2):
                j = 2 * jj + e
                g, t = divmod(j, 4)
                nc.vector.tensor_scalar(
                    out=mv_raw[1][g][1][:, t, cols],
                    in0=bank[:, e * 256 : (e + 1) * 256],
                    scalar1=limits[:, g, 4 + t : 5 + t],
                    scalar2=limits[:, g, t : t + 1],
                    op0=ALU.min,
                    op1=ALU.max,
                )

        def out_pair(c, part, copy):
            bank = new_bank()
            s0 = HALF + 256 * part
            for i in range(2):
                for m in range(2):
                    for g in range(2):
                        out_pass(bank[:, i * 256 : (i + 1) * 256], 2 * c + i, s0, 256, m, g)
            res = work.tile([P, HALF], F32, name="res", tag="res", bufs=6)
            copy(out=res[:], in_=bank[:])
            nc.sync.dma_start(
                out=out[256 * c : 256 * (c + 1), s0 : s0 + 256].rearrange("(i p) s -> p i s", i=2),
                in_=res[:].rearrange("p (i s) -> p i s", i=2),
            )

        il_dev(0)
        droop_bank(0, 0)
        droop_bank(0, 1)
        q_dev(0)
        droop_quant(0)
        droop_bank(1, 0)
        droop_bank(1, 1)
        limits_step()
        permute(0, 0)
        droop_quant(1)
        permute_plane(0, 0)
        for j in range(8):
            d_bank(j, 0)
            if j == 2:
                permute(0, 1)
                permute_plane(0, 1)
        rx_unit(0, 0)
        rx_unit(0, 1)
        for g in range(2):
            permute(1, g)
            permute_plane(1, g)
        rx_unit(1, 0)
        il_mv(1, 0, 0)
        il_mv(1, 1, 0)
        q_mv(1, 0, 0)
        q_mv(1, 1, 0)
        rx_unit(1, 1)
        il_mv(0, 0, 0)
        il_dev(1)
        q_mv(0, 0, 0)
        q_dev(1)
        rx_unit(0, 2)
        il_mv(0, 1, 0)
        rx_join(0, 0)
        q_mv(0, 1, 0)
        rx_join(1, 0)
        rx_quant(0, 0)
        rx_quant(1, 0)
        rx_unit(1, 2)
        for b in range(4):
            if b < 2:
                d_pair(2 * b, 0)
                d_pair(2 * b + 1, 0)
            rx_bank(b // 2, 3, b % 2, 0)
            rx_bank(b // 2, 3, b % 2, 1)
            out_bank(b, 0, HALF, scopy, nc.sync)
            if b >= 2:
                il_mv(0, b - 2, 1, scopy, 0)
            if b < 2:
                rx_join(0, 1 + b)
                rx_join(1, 1 + b)
                rx_quant(0, 1 + b)
                rx_quant(1, 1 + b)
            if b == 2:
                rx_join(0, 3)
                for g in range(2):
                    il_mv(1, g, 1, vcopy, 0)
                rx_quant(0, 3)
                for g in range(2):
                    q_mv(1, g, 1, 0)
        rx_join(1, 3)
        q_mv(0, 0, 1, 0)
        rx_quant(1, 3)
        q_mv(0, 1, 1, 0)
        for b in range(4, 8):
            d_pair(b - 4, 1)
            out_bank(b, 0, HALF, scopy, nc.sync)
            if b < 6:
                il_mv(0, b - 4, 1, scopy, 1)
        for g in range(2):
            il_mv(1, g, 1, vcopy, 1)
        for g in range(2):
            q_mv(0, g, 1, 1)
            q_mv(1, g, 1, 1)
        for c in range(4):
            out_pair(c, 0, scopy)
        for c in range(3):
            out_pair(c, 1, scopy if c % 2 == 0 else vcopy)
        out_bank(6, HALF + 256, 256, vcopy, nc.sync)
        out_bank(7, HALF + 256, 256, scopy, nc.scalar)
